import numpy as np
import ml_dtypes


def mxq(x, axis, fmt="e4m3"):
    dtype, down = {"e4m3": (ml_dtypes.float8_e4m3fn, 7), "e5m2": (ml_dtypes.float8_e5m2, 14)}[fmt]
    v = np.moveaxis(np.asarray(x, np.float32).astype(ml_dtypes.bfloat16).astype(np.float64), axis, -1)
    blocks = v.reshape(v.shape[:-1] + (-1, 32))
    amax = np.abs(blocks).max(-1, keepdims=True)
    byte = np.maximum(np.where(amax > 0, np.frexp(amax)[1] - 1 + 127, 0) - down, 1)
    scale = np.exp2(byte - 127.0)
    codes = (blocks / scale).astype(np.float32).astype(dtype).astype(np.float64)
    return np.moveaxis((codes * scale).reshape(v.shape), -1, axis)


WIDE = False


def mx_kscale(k):
    if not WIDE:
        return np.ones(k)
    levels = np.array([10, -10, 5, -5, 0])
    if k % 512:
        return np.exp2(np.random.permutation(np.resize(levels, k // 32))).repeat(32)
    a = np.empty((k // 512, 16))
    for p in range(k // 512):
        a[p, :8] = np.random.permutation(np.resize(levels, 8))
        for g in range(8):
            far = levels[np.abs(levels - a[p, g]) >= 10]
            a[p, g + 8] = far[np.random.randint(len(far))]
    return np.exp2(a.ravel()).repeat(32)


def f64(x):
    return np.asarray(x).astype(np.float64)


def striped(idx):
    return np.tile(idx.reshape(-1, 16).T, (8, 1)).astype(np.uint16)


def unstriped(offs):
    return offs[:16].T.reshape(-1).astype(np.int64)


def striped8(idx):
    return np.concatenate([x.reshape(-1, 16).T for x in idx]).astype(np.uint16)


def runs(offs, k):
    lists = np.stack([offs[16 * r : 16 * r + 16].T.reshape(-1) for r in range(8)]).astype(np.int64)
    return lists[np.arange(k) % 512 // 64]


def pack_weight(w):
    k, n = w.shape
    w = f64(np.asarray(w, np.float32).astype(ml_dtypes.bfloat16)).reshape(k // 32, 32, n)
    amax = np.abs(w).max(1)
    byte = np.clip(np.where(amax > 0, np.frexp(amax)[1] - 1 + 127 - 7, 1), 1, 254)
    scaled = (w * np.exp2(127.0 - byte)[:, None, :]).reshape(k, n).astype(np.float32)
    words = np.ascontiguousarray(scaled.reshape(k // 512, 128, 4, n).transpose(0, 1, 3, 2)).astype(ml_dtypes.float8_e4m3fn).view(np.uint8)
    return words, np.ascontiguousarray(byte.astype(np.uint8).reshape(k // 512, 16, n))


def unpack_weight(words, scales):
    g, p, n, _ = words.shape
    vals = np.ascontiguousarray(words).view(ml_dtypes.float8_e4m3fn).astype(np.float64) * np.repeat(np.exp2(scales.astype(np.float64) - 127.0), 8, axis=1)[..., None]
    return vals.transpose(0, 1, 3, 2).reshape(g * 512, n)


def sigmoid(v):
    return 1.0 / (1.0 + np.exp(-np.maximum(v, -700.0)))

def planes(y):
    n, m = y.shape
    v = y.astype(np.float32).astype(ml_dtypes.bfloat16).astype(np.float64).reshape(n // 32, 32, m)
    top = np.abs(v).max(1)
    byte = np.clip(np.where(top > 0, np.frexp(top)[1] - 1 + 127 - 7, 1), 1, 254)
    codes = (v * np.exp2(127.0 - byte)[:, None, :]).reshape(n, m).astype(np.float32).astype(ml_dtypes.float8_e4m3fn).view(np.uint8)
    words = codes.reshape(n // 512, 128, 4, m).transpose(0, 1, 3, 2)
    return np.ascontiguousarray(words), np.ascontiguousarray(byte.astype(np.uint8).reshape(n // 512, 16, m))


K, T, S, N, G, H = 512, 2048, 512, 512, 2048, 512


def setup_inputs():
    n = np.random.standard_normal
    s = mx_kscale(K)[:, None]
    u = mx_kscale(S)
    packed_xT = pack_weight(n((K, T)) * s)
    packed_dT = pack_weight(n((K, G)) / s)
    packed_w1 = pack_weight(n((H, N)) / np.sqrt(H) / u[:, None])
    return {
        "x_words": packed_xT[0],
        "x_scales": packed_xT[1],
        "d_words": packed_dT[0],
        "d_scales": packed_dT[1],
        "gn": (np.random.uniform(0.5, 1.5, (H, 1)) * u[:, None]).astype(np.float32),
        "w1_words": packed_w1[0],
        "w1_scales": packed_w1[1],
        "offs": striped(np.random.permutation(T)[:S]),
        "kidx": striped8(np.random.randint(0, G, (8, H))),
        "n1": striped8(np.stack([np.random.permutation(S) for _ in range(8)])),
        "n2": striped8(np.stack([np.random.permutation(S) for _ in range(8)])),
    }


def reference(x_words, x_scales, d_words, d_scales, gn, w1_words, w1_scales, offs, kidx, n1, n2):
    d_kidx = unpack_weight(d_words, d_scales)[np.arange(K)[:, None], runs(kidx, K)]
    xq = unpack_weight(x_words, x_scales)[:, unstriped(offs)]
    s = 0.0625 * (d_kidx.T @ xq)
    st = s - (s[np.arange(H)[:, None], runs(n1, H)])
    z = f64(gn) * (st - (0.5 * (st[np.arange(H)[:, None], runs(n1, H)])))
    h = unpack_weight(w1_words, w1_scales).T @ mxq(z, 0, "e4m3")
    st2 = h * (sigmoid(h[np.arange(N)[:, None], runs(n2, N)]))
    out_0 = np.maximum(st2, st2[np.arange(N)[:, None], runs(n2, N)])
    return (out_0,) + planes(out_0)

@@ -1,0 +1,221 @@
+from contextlib import ExitStack
+
+import concourse.mybir as mybir
+
+K, T, S, N, G, H = 512, 2048, 512, 512, 2048, 512
+FLOPS = 2 * K * H * S + 2 * H * N * S
+
+F32 = mybir.dt.float32
+BF16 = mybir.dt.bfloat16
+I32 = mybir.dt.int32
+U32 = mybir.dt.uint32
+U16 = mybir.dt.uint16
+U8 = mybir.dt.uint8
+FP8X4 = mybir.dt.float8_e4m3fn_x4
+ACT = mybir.ActivationFunctionType
+ALU = mybir.AluOpType
+
+P = 128
+PACK = 4
+HALF = S // 2
+HALVES = 2
+LIST_COLS = HALF // 16
+
+
+def words_view(dram_words):
+    return dram_words[0].rearrange("p n t -> p (n t)").bitcast(I32)
+
+
+def tile_picked_keytwicetwicp_none_po_kernel(
+    tc, x_words, x_scales, d_words, d_scales, gn, w1_words, w1_scales, offs, kidx, n1, n2, out_0, out_1, out_2
+):
+    nc = tc.nc
+    with ExitStack() as ctx:
+        pool = ctx.enter_context(tc.tile_pool(name="sbuf", bufs=1))
+        psum = ctx.enter_context(tc.psum_pool(name="psum", bufs=1))
+
+        def sb(name, shape, dtype, tag=None):
+            return pool.tile(shape, dtype, name=name, tag=tag or name, align_bytes=64)
+
+        def cols(c):
+            return slice(c * HALF, (c + 1) * HALF)
+
+        def list_half(lst, c):
+            return lst[:, c * LIST_COLS : (c + 1) * LIST_COLS]
+
+        def deal(dst, src):
+            nc.vector.tensor_copy(
+                out=dst[:].rearrange("p (t m) -> p m t", t=PACK), in_=src[:].rearrange("p (m t) -> p m t", t=PACK)
+            )
+
+        def interleave_views(dst, src):
+            return (
+                dst[:].rearrange("p (c i t) -> p c t i", i=4, t=PACK),
+                src.rearrange("p t (c i) -> p c t i", i=4),
+            )
+
+        kidx_sb = sb("kidx_sb", [P, H // 16], U16)
+        offs_sb = sb("offs_sb", [P, S // 16], U16)
+        n1_sb = sb("n1_sb", [P, S // 16], U16)
+        n2_sb = sb("n2_sb", [P, S // 16], U16)
+        d_tab = sb("d_tab", [P, G], U32)
+        x_tab = sb("x_tab", [P, T], U32)
+        ds_tab = sb("ds_tab", [P, G], U8)
+        xs_tab = sb("xs_tab", [P, T], U8)
+        ws_raw = sb("ws_raw", [P, N], U8)
+        gn_sb = sb("gn_sb", [P, PACK], F32)
+
+        nc.vector.memset(ds_tab[:].bitcast(I32), 0)
+        nc.vector.memset(xs_tab[:].bitcast(I32), 0)
+        nc.vector.memset(ws_raw[:].bitcast(I32), 0)
+
+        nc.sync.dma_start(kidx_sb[:], kidx)
+        nc.sync.dma_start(offs_sb[:], offs)
+        nc.sync.dma_start(n1_sb[:], n1)
+        nc.sync.dma_start(n2_sb[:], n2)
+        nc.sync.dma_start(gn_sb[:], gn.rearrange("(p t) o -> p (t o)", t=PACK))
+        d_rows = d_scales[0].rearrange("(a r) c -> r a c", r=2)
+        for r in range(2):
+            nc.sync.dma_start(ds_tab[r:P:16, :].bitcast(I32), d_rows[r].bitcast(I32))
+        nc.sync.dma_start(d_tab[:].bitcast(I32), words_view(d_words))
+        for q in range(4):
+            nc.scalar.dma_start(xs_tab[32 * q : 32 * q + 4, :].bitcast(I32), x_scales[0, 4 * q : 4 * q + 4, :].bitcast(I32))
+        nc.sync.dma_start(x_tab[:].bitcast(I32), words_view(x_words))
+        for q in range(4):
+            nc.sync.dma_start(ws_raw[32 * q : 32 * q + 4, :].bitcast(I32), w1_scales[0, 4 * q : 4 * q + 4, :].bitcast(I32))
+        warm = sb("warm", [P, PACK], F32)
+        nc.scalar.activation(warm[:], gn_sb[:], ACT.Sigmoid)
+
+        ds_got = sb("ds_got", [P, H], U8)
+        nc.vector.tensor_copy(ds_got[:], ds_tab[:].indirect(kidx_sb[:]))
+        ds_dealt = sb("ds_dealt", [P, H], U8)
+        deal(ds_dealt, ds_got)
+        for r in range(2):
+            nc.scalar.dma_start(ds_dealt[2 + r : P : 32, :].bitcast(I32), ds_dealt[16 + r : P : 32, :].bitcast(I32))
+        w_raw = sb("w_raw", [P, N], U32, tag="ds_tab")
+        nc.sync.dma_start(w_raw[:].bitcast(I32), words_view(w1_words))
+        xs_got = sb("xs_got", [P, S], U8)
+        nc.vector.tensor_copy(xs_got[:], xs_tab[:].indirect(offs_sb[:]))
+        d_got = sb("d_got", [P, H], U32)
+        nc.vector.tensor_copy(d_got[:], d_tab[:].indirect(kidx_sb[:]))
+        d_dealt = sb("d_dealt", [P, H], U32)
+        deal(d_dealt, d_got)
+        x_got = [sb("x_got%d" % c, [P, HALF], U32) for c in range(HALVES)]
+        for c in range(HALVES):
+            nc.vector.tensor_copy(x_got[c][:], x_tab[:].indirect(list_half(offs_sb, c)))
+
+        row_scale = sb("row_scale", [P, PACK], F32)
+        nc.scalar.activation(row_scale[:], gn_sb[:], ACT.Copy, scale=0.03125)
+
+        def bank(t, c):
+            return psum.tile([P, HALF], F32, name="bank%d_%d" % (t, c), tag="bank%d_%d" % (t, c))
+
+        s_ps = {}
+        for c in range(HALVES):
+            for t in range(PACK):
+                s_ps[t, c] = bank(t, c)
+                nc.tensor.matmul_mx(
+                    out=s_ps[t, c][:],
+                    lhsT=d_dealt[:, t * P : (t + 1) * P].bitcast(FP8X4),
+                    lhsT_scale=ds_dealt[:, t * P : (t + 1) * P],
+                    rhs=x_got[c][:].bitcast(FP8X4),
+                    rhs_scale=xs_got[:, cols(c)],
+                    start=True,
+                    stop=True,
+                )
+
+        w_dealt = sb("w_dealt", [P, N], U32)
+        ws_dealt = sb("ws_dealt", [P, N], U8)
+        deal(w_dealt, w_raw)
+        deal(ws_dealt, ws_raw)
+
+        s_tiles = [sb("s_win%d" % t, [P, S if t == 0 else 2 * S], F32) for t in range(PACK)]
+        s_last = sb("s_last", [P, S], F32)
+        s_win = [s_tiles[t][:, :S] for t in range(PACK)]
+        s_dup = [s_tiles[t + 1][:, S:] for t in range(PACK - 1)] + [s_last[:]]
+        m_win = [sb("m_win%d" % t, [P, S], F32) for t in range(PACK)]
+        m_dbl = [sb("m_dbl%d" % t, [P, S], F32) for t in range(PACK)]
+        for t in range(PACK):
+            for c in range(HALVES):
+                for dst in (s_win, s_dup):
+                    nc.scalar.activation(dst[t][:, cols(c)], s_ps[t, c][:], ACT.Copy, scale=row_scale[:, t : t + 1])
+            if t == 0:
+                for c in range(HALVES):
+                    nc.vector.tensor_tensor(
+                        m_win[t][:, cols(c)], s_tiles[t][:].indirect(list_half(n1_sb, c)), s_dup[t][:, cols(c)], ALU.subtract
+                    )
+            else:
+                nc.vector.tensor_tensor(m_win[t][:], s_tiles[t][:].indirect(n1_sb[:]), s_dup[t], ALU.subtract)
+        for c in range(HALVES):
+            for t in range(PACK):
+                nc.scalar.activation(m_dbl[t][:, cols(c)], m_win[t][:, cols(c)], ACT.Copy, scale=2.0)
+
+        h_ps = [psum.tile([P, S], F32, name="h_ps%d" % t, tag="bank%d_0" % t) for t in range(PACK)]
+        h_win = [sb("h_win%d" % t, [P, S], F32) for t in range(PACK)]
+        for c in range(HALVES):
+            z = sb("z%d" % c, [P, PACK, HALF], F32)
+            for t in range(PACK):
+                nc.vector.tensor_tensor(
+                    z[:, t, :], m_win[t][:].indirect(list_half(n1_sb, c)), m_dbl[t][:, cols(c)], ALU.subtract
+                )
+            z_bf = sb("z_bf%d" % c, [P, HALF * PACK], BF16)
+            dst, src = interleave_views(z_bf, z[:])
+            if c == 0:
+                nc.scalar.copy(dst, src)
+            else:
+                nc.vector.tensor_copy(dst, src)
+            z_codes = sb("z_codes%d" % c, [P, HALF], U32)
+            z_scales = sb("z_scales%d" % c, [P, HALF], U8)
+            nc.vector.quantize_mx(out=z_codes[:].bitcast(FP8X4), scales=z_scales[:], in_=z_bf[:])
+            for t in range(PACK):
+                nc.tensor.matmul_mx(
+                    out=h_ps[t][:, cols(c)],
+                    lhsT=w_dealt[:, t * P : (t + 1) * P].bitcast(FP8X4),
+                    lhsT_scale=ws_dealt[:, t * P : (t + 1) * P],
+                    rhs=z_codes[:].bitcast(FP8X4),
+                    rhs_scale=z_scales[:],
+                    start=True,
+                    stop=True,
+                )
+                if c == 0:
+                    nc.scalar.copy(h_win[t][:, cols(c)], h_ps[t][:, cols(c)])
+
+        y = sb("y", [P, PACK, S], F32)
+        out_rows = out_0.rearrange("(p t) j -> p t j", t=PACK)
+        for t in range(PACK):
+            nc.scalar.copy(h_win[t][:, cols(1)], h_ps[t][:, cols(1)])
+            both = sb("both%d" % t, [P, 2 * S], F32)
+            st2, gate = both[:, :S], both[:, S:]
+            other = sb("other%d" % t, [P, S], F32)
+            for c in range(HALVES):
+                nc.scalar.activation(gate[:, cols(c)], h_win[t][:].indirect(list_half(n2_sb, c)), ACT.Sigmoid)
+            if t == 0:
+                for c in range(HALVES):
+                    nc.vector.tensor_tensor(st2[:, cols(c)], h_ps[t][:, cols(c)], gate[:, cols(c)], ALU.mult)
+            else:
+                nc.vector.tensor_tensor(st2, h_ps[t][:], gate, ALU.mult)
+            if t < PACK - 1:
+                nc.vector.tensor_copy(other[:], both[:].indirect(n2_sb[:]))
+                nc.vector.tensor_tensor(y[:, t, :], st2, other[:], ALU.max)
+                nc.sync.dma_start(out_rows[:, t, :], y[:, t, :])
+            else:
+                for c in range(HALVES):
+                    nc.vector.tensor_copy(other[:, cols(c)], both[:].indirect(list_half(n2_sb, c)))
+                for c in range(HALVES):
+                    nc.vector.tensor_tensor(y[:, t, cols(c)], st2[:, cols(c)], other[:, cols(c)], ALU.max)
+                    nc.sync.dma_start(out_rows[:, t, cols(c)], y[:, t, cols(c)])
+
+        y_scales = sb("y_scales", [P, S], U8)
+        for c in range(HALVES):
+            y_bf = sb("y_bf%d" % c, [P, HALF * PACK], BF16)
+            dst, src = interleave_views(y_bf, y[:, :, cols(c)])
+            if c == 0:
+                nc.scalar.copy(dst, src)
+            else:
+                nc.vector.tensor_copy(dst, src)
+            y_codes = sb("y_codes%d" % c, [P, HALF], U32)
+            nc.vector.quantize_mx(out=y_codes[:].bitcast(FP8X4), scales=y_scales[:, cols(c)], in_=y_bf[:])
+            nc.sync.dma_start(words_view(out_1)[:, cols(c)], y_codes[:].bitcast(I32))
+        for q in range(4):
+            eng = nc.scalar if q % 2 == 0 else nc.sync
+            eng.dma_start(out_2[0, 4 * q : 4 * q + 4, :].bitcast(I32), y_scales[32 * q : 32 * q + 4, :].bitcast(I32))

@@ -32,6 +32,7 @@ def tile_picked_keytwicetwicp_none_po_kernel(
     nc = tc.nc
     with ExitStack() as ctx:
         pool = ctx.enter_context(tc.tile_pool(name="sbuf", bufs=1))
+        reuse = ctx.enter_context(tc.tile_pool(name="reuse", bufs=1))
         psum = ctx.enter_context(tc.psum_pool(name="psum", bufs=1))
 
         def sb(name, shape, dtype, tag=None):
@@ -59,15 +60,15 @@ def tile_picked_keytwicetwicp_none_po_kernel(
         n1_sb = sb("n1_sb", [P, S // 16], U16)
         n2_sb = sb("n2_sb", [P, S // 16], U16)
         d_tab = sb("d_tab", [P, G], U32)
-        x_tab = sb("x_tab", [P, T], U32)
+        x_tab = reuse.tile([P, T], U32, name="x_tab", align_bytes=64, offset=0)
         ds_tab = sb("ds_tab", [P, G], U8)
         xs_tab = sb("xs_tab", [P, T], U8)
-        ws_raw = sb("ws_raw", [P, N], U8)
         gn_sb = sb("gn_sb", [P, PACK], F32)
 
         nc.vector.memset(ds_tab[:].bitcast(I32), 0)
-        nc.vector.memset(xs_tab[:].bitcast(I32), 0)
-        nc.vector.memset(ws_raw[:].bitcast(I32), 0)
+        nc.gpsimd.memset(xs_tab[:].bitcast(I32), 0)
+        ws_raw = sb("ws_raw", [P, N], U8)
+        nc.gpsimd.memset(ws_raw[:].bitcast(I32), 0)
 
         nc.sync.dma_start(kidx_sb[:], kidx)
         nc.sync.dma_start(offs_sb[:], offs)
@@ -79,7 +80,7 @@ def tile_picked_keytwicetwicp_none_po_kernel(
             nc.sync.dma_start(ds_tab[r:P:16, :].bitcast(I32), d_rows[r].bitcast(I32))
         nc.sync.dma_start(d_tab[:].bitcast(I32), words_view(d_words))
         for q in range(4):
-            nc.scalar.dma_start(xs_tab[32 * q : 32 * q + 4, :].bitcast(I32), x_scales[0, 4 * q : 4 * q + 4, :].bitcast(I32))
+            nc.sync.dma_start(xs_tab[32 * q : 32 * q + 4, :].bitcast(I32), x_scales[0, 4 * q : 4 * q + 4, :].bitcast(I32))
         nc.sync.dma_start(x_tab[:].bitcast(I32), words_view(x_words))
         for q in range(4):
             nc.sync.dma_start(ws_raw[32 * q : 32 * q + 4, :].bitcast(I32), w1_scales[0, 4 * q : 4 * q + 4, :].bitcast(I32))
@@ -98,34 +99,41 @@ def tile_picked_keytwicetwicp_none_po_kernel(
         nc.vector.tensor_copy(xs_got[:], xs_tab[:].indirect(offs_sb[:]))
         d_got = sb("d_got", [P, H], U32)
         nc.vector.tensor_copy(d_got[:], d_tab[:].indirect(kidx_sb[:]))
-        d_dealt = sb("d_dealt", [P, H], U32)
-        deal(d_dealt, d_got)
-        x_got = [sb("x_got%d" % c, [P, HALF], U32) for c in range(HALVES)]
+        d_first = sb("d_first", [P, P], U32)
+        d_by_slot = d_got[:].rearrange("p (m t) -> p m t", t=PACK)
+        nc.vector.tensor_copy(d_first[:], d_by_slot[:, :, 0])
+        x_got = sb("x_got", [P, S], U32)
         for c in range(HALVES):
-            nc.vector.tensor_copy(x_got[c][:], x_tab[:].indirect(list_half(offs_sb, c)))
+            nc.vector.tensor_copy(x_got[:, cols(c)], x_tab[:].indirect(list_half(offs_sb, c)))
+        d_rest = reuse.tile([P, PACK - 1, P], U32, name="d_rest", align_bytes=64, offset=5 * N)
+        nc.vector.tensor_copy(d_rest[:].rearrange("p t m -> p m t"), d_by_slot[:, :, 1:])
+        d_stat = [d_first[:]] + [d_rest[:, t, :] for t in range(PACK - 1)]
 
         row_scale = sb("row_scale", [P, PACK], F32)
         nc.scalar.activation(row_scale[:], gn_sb[:], ACT.Copy, scale=0.03125)
 
-        def bank(t, c):
-            return psum.tile([P, HALF], F32, name="bank%d_%d" % (t, c), tag="bank%d_%d" % (t, c))
+        s_first = psum.tile([P, HALF], F32, name="s_first")
+        s_banks = [psum.tile([P, S], F32, name="s_bank%d" % t, tag="bank%d" % t) for t in range(PACK)]
+        s_ps = {(0, 0): s_first[:], (0, 1): s_banks[0][:, cols(1)]}
 
-        s_ps = {}
+        def scores(out, t, js):
+            nc.tensor.matmul_mx(
+                out=out,
+                lhsT=d_stat[t].bitcast(FP8X4),
+                lhsT_scale=ds_dealt[:, t * P : (t + 1) * P],
+                rhs=x_got[:, js].bitcast(FP8X4),
+                rhs_scale=xs_got[:, js],
+                start=True,
+                stop=True,
+            )
+
         for c in range(HALVES):
-            for t in range(PACK):
-                s_ps[t, c] = bank(t, c)
-                nc.tensor.matmul_mx(
-                    out=s_ps[t, c][:],
-                    lhsT=d_dealt[:, t * P : (t + 1) * P].bitcast(FP8X4),
-                    lhsT_scale=ds_dealt[:, t * P : (t + 1) * P],
-                    rhs=x_got[c][:].bitcast(FP8X4),
-                    rhs_scale=xs_got[:, cols(c)],
-                    start=True,
-                    stop=True,
-                )
+            scores(s_ps[0, c], 0, cols(c))
+        for t in range(1, PACK):
+            scores(s_banks[t][:], t, slice(0, S))
 
-        w_dealt = sb("w_dealt", [P, N], U32)
-        ws_dealt = sb("ws_dealt", [P, N], U8)
+        w_dealt = reuse.tile([P, N], U32, name="w_dealt", align_bytes=64, offset=0)
+        ws_dealt = reuse.tile([P, N], U8, name="ws_dealt", align_bytes=64, offset=4 * N)
         deal(w_dealt, w_raw)
         deal(ws_dealt, ws_raw)
 
@@ -134,11 +142,15 @@ def tile_picked_keytwicetwicp_none_po_kernel(
         s_win = [s_tiles[t][:, :S] for t in range(PACK)]
         s_dup = [s_tiles[t + 1][:, S:] for t in range(PACK - 1)] + [s_last[:]]
         m_win = [sb("m_win%d" % t, [P, S], F32) for t in range(PACK)]
-        m_dbl = [sb("m_dbl%d" % t, [P, S], F32) for t in range(PACK)]
         for t in range(PACK):
-            for c in range(HALVES):
+            scale = row_scale[:, t : t + 1]
+            if t == 0:
+                for c in range(HALVES):
+                    for dst in (s_win, s_dup):
+                        nc.scalar.activation(dst[t][:, cols(c)], s_ps[t, c], ACT.Copy, scale=scale)
+            else:
                 for dst in (s_win, s_dup):
-                    nc.scalar.activation(dst[t][:, cols(c)], s_ps[t, c][:], ACT.Copy, scale=row_scale[:, t : t + 1])
+                    nc.scalar.activation(dst[t], s_banks[t][:], ACT.Copy, scale=scale)
             if t == 0:
                 for c in range(HALVES):
                     nc.vector.tensor_tensor(
@@ -146,17 +158,35 @@ def tile_picked_keytwicetwicp_none_po_kernel(
                     )
             else:
                 nc.vector.tensor_tensor(m_win[t][:], s_tiles[t][:].indirect(n1_sb[:]), s_dup[t], ALU.subtract)
-        for c in range(HALVES):
-            for t in range(PACK):
-                nc.scalar.activation(m_dbl[t][:, cols(c)], m_win[t][:, cols(c)], ACT.Copy, scale=2.0)
+        m_dbl = {}
 
-        h_ps = [psum.tile([P, S], F32, name="h_ps%d" % t, tag="bank%d_0" % t) for t in range(PACK)]
+        def double(t, c, dst):
+            m_dbl[t, c] = dst
+            nc.scalar.activation(dst, m_win[t][:, cols(c)], ACT.Copy, scale=2.0)
+
+        for c, t in [(0, 0), (0, 1), (0, 2), (0, 3), (1, 0), (1, 1)]:
+            double(t, c, sb("m_dbl%d_%d" % (t, c), [P, HALF], F32)[:])
+
+        h_ps = [psum.tile([P, S], F32, name="h_ps%d" % t, tag="bank%d" % ((t + 4) % 7)) for t in range(PACK)]
         h_win = [sb("h_win%d" % t, [P, S], F32) for t in range(PACK)]
+        both = [sb("both%d" % t, [P, 2 * S], F32) for t in range(PACK)]
+
+        def leave_bank(t, c):
+            if t == 0:
+                nc.scalar.activation(h_win[t][:, cols(c)], h_ps[t][:, cols(c)], ACT.Sigmoid)
+                nc.scalar.copy(both[t][:, S:][:, cols(c)], h_ps[t][:, cols(c)])
+            else:
+                nc.scalar.copy(h_win[t][:, cols(c)], h_ps[t][:, cols(c)])
+
         for c in range(HALVES):
             z = sb("z%d" % c, [P, PACK, HALF], F32)
+            if c == 1:
+                m_late = sb("m_late", [P, 2, HALF], F32, tag="z0")
+                for t in (2, 3):
+                    double(t, c, m_late[:, t - 2, :])
             for t in range(PACK):
                 nc.vector.tensor_tensor(
-                    z[:, t, :], m_win[t][:].indirect(list_half(n1_sb, c)), m_dbl[t][:, cols(c)], ALU.subtract
+                    z[:, t, :], m_win[t][:].indirect(list_half(n1_sb, c)), m_dbl[t, c], ALU.subtract
                 )
             z_bf = sb("z_bf%d" % c, [P, HALF * PACK], BF16)
             dst, src = interleave_views(z_bf, z[:])
@@ -178,29 +208,30 @@ def tile_picked_keytwicetwicp_none_po_kernel(
                     stop=True,
                 )
                 if c == 0:
-                    nc.scalar.copy(h_win[t][:, cols(c)], h_ps[t][:, cols(c)])
+                    leave_bank(t, c)
 
         y = sb("y", [P, PACK, S], F32)
         out_rows = out_0.rearrange("(p t) j -> p t j", t=PACK)
         for t in range(PACK):
-            nc.scalar.copy(h_win[t][:, cols(1)], h_ps[t][:, cols(1)])
-            both = sb("both%d" % t, [P, 2 * S], F32)
-            st2, gate = both[:, :S], both[:, S:]
+            leave_bank(t, 1)
+            st2, gate = both[t][:, :S], both[t][:, S:]
             other = sb("other%d" % t, [P, S], F32)
-            for c in range(HALVES):
-                nc.scalar.activation(gate[:, cols(c)], h_win[t][:].indirect(list_half(n2_sb, c)), ACT.Sigmoid)
             if t == 0:
                 for c in range(HALVES):
-                    nc.vector.tensor_tensor(st2[:, cols(c)], h_ps[t][:, cols(c)], gate[:, cols(c)], ALU.mult)
+                    nc.vector.tensor_tensor(
+                        st2[:, cols(c)], h_win[t][:].indirect(list_half(n2_sb, c)), gate[:, cols(c)], ALU.mult
+                    )
             else:
+                for c in range(HALVES):
+                    nc.scalar.activation(gate[:, cols(c)], h_win[t][:].indirect(list_half(n2_sb, c)), ACT.Sigmoid)
                 nc.vector.tensor_tensor(st2, h_ps[t][:], gate, ALU.mult)
             if t < PACK - 1:
-                nc.vector.tensor_copy(other[:], both[:].indirect(n2_sb[:]))
+                nc.vector.tensor_copy(other[:], both[t][:].indirect(n2_sb[:]))
                 nc.vector.tensor_tensor(y[:, t, :], st2, other[:], ALU.max)
                 nc.sync.dma_start(out_rows[:, t, :], y[:, t, :])
             else:
                 for c in range(HALVES):
-                    nc.vector.tensor_copy(other[:, cols(c)], both[:].indirect(list_half(n2_sb, c)))
+                    nc.vector.tensor_copy(other[:, cols(c)], both[t][:].indirect(list_half(n2_sb, c)))
                 for c in range(HALVES):
                     nc.vector.tensor_tensor(y[:, t, cols(c)], st2[:, cols(c)], other[:, cols(c)], ALU.max)
                     nc.sync.dma_start(out_rows[:, t, cols(c)], y[:, t, cols(c)])

@@ -67,8 +67,6 @@ def tile_picked_keytwicetwicp_none_po_kernel(
 
         nc.vector.memset(ds_tab[:].bitcast(I32), 0)
         nc.gpsimd.memset(xs_tab[:].bitcast(I32), 0)
-        ws_raw = sb("ws_raw", [P, N], U8)
-        nc.gpsimd.memset(ws_raw[:].bitcast(I32), 0)
 
         nc.sync.dma_start(kidx_sb[:], kidx)
         nc.sync.dma_start(offs_sb[:], offs)
@@ -82,8 +80,6 @@ def tile_picked_keytwicetwicp_none_po_kernel(
         for q in range(4):
             nc.sync.dma_start(xs_tab[32 * q : 32 * q + 4, :].bitcast(I32), x_scales[0, 4 * q : 4 * q + 4, :].bitcast(I32))
         nc.sync.dma_start(x_tab[:].bitcast(I32), words_view(x_words))
-        for q in range(4):
-            nc.sync.dma_start(ws_raw[32 * q : 32 * q + 4, :].bitcast(I32), w1_scales[0, 4 * q : 4 * q + 4, :].bitcast(I32))
         warm = sb("warm", [P, PACK], F32)
         nc.scalar.activation(warm[:], gn_sb[:], ACT.Sigmoid)
 
@@ -93,12 +89,16 @@ def tile_picked_keytwicetwicp_none_po_kernel(
         deal(ds_dealt, ds_got)
         for r in range(2):
             nc.scalar.dma_start(ds_dealt[2 + r : P : 32, :].bitcast(I32), ds_dealt[16 + r : P : 32, :].bitcast(I32))
-        w_raw = sb("w_raw", [P, N], U32, tag="ds_tab")
-        nc.sync.dma_start(w_raw[:].bitcast(I32), words_view(w1_words))
+        ws_raw = sb("ws_raw", [P, N], U8, tag="ds_got")
+        nc.gpsimd.memset(ws_raw[:].bitcast(I32), 0)
+        for q in range(4):
+            nc.sync.dma_start(ws_raw[32 * q : 32 * q + 4, :].bitcast(I32), w1_scales[0, 4 * q : 4 * q + 4, :].bitcast(I32))
         xs_got = sb("xs_got", [P, S], U8)
         nc.vector.tensor_copy(xs_got[:], xs_tab[:].indirect(offs_sb[:]))
         d_got = sb("d_got", [P, H], U32)
         nc.vector.tensor_copy(d_got[:], d_tab[:].indirect(kidx_sb[:]))
+        w_raw = sb("w_raw", [P, N], U32, tag="d_tab")
+        nc.sync.dma_start(w_raw[:].bitcast(I32), words_view(w1_words))
         d_first = sb("d_first", [P, P], U32)
         d_by_slot = d_got[:].rearrange("p (m t) -> p m t", t=PACK)
         nc.vector.tensor_copy(d_first[:], d_by_slot[:, :, 0])
@@ -164,12 +164,14 @@ def tile_picked_keytwicetwicp_none_po_kernel(
             m_dbl[t, c] = dst
             nc.scalar.activation(dst, m_win[t][:, cols(c)], ACT.Copy, scale=2.0)
 
-        for c, t in [(0, 0), (0, 1), (0, 2), (0, 3), (1, 0), (1, 1)]:
-            double(t, c, sb("m_dbl%d_%d" % (t, c), [P, HALF], F32)[:])
+        both = [sb("both%d" % t, [P, 2 * S if t < PACK - 1 else S], F32) for t in range(PACK)]
+        for t in range(PACK):
+            double(t, 0, both[1 + t // 2][:, S:][:, cols(t % 2)])
+        for t in range(2):
+            double(t, 1, sb("m_dbl%d" % t, [P, HALF], F32)[:])
 
         h_ps = [psum.tile([P, S], F32, name="h_ps%d" % t, tag="bank%d" % ((t + 4) % 7)) for t in range(PACK)]
         h_win = [sb("h_win%d" % t, [P, S], F32) for t in range(PACK)]
-        both = [sb("both%d" % t, [P, 2 * S], F32) for t in range(PACK)]
 
         def leave_bank(t, c):
             if t == 0:
@@ -212,29 +214,34 @@ def tile_picked_keytwicetwicp_none_po_kernel(
 
         y = sb("y", [P, PACK, S], F32)
         out_rows = out_0.rearrange("(p t) j -> p t j", t=PACK)
-        for t in range(PACK):
+        st2 = [both[t][:, :S] for t in range(PACK)]
+        other = [sb("other%d" % t, [P, S], F32) for t in range(PACK)]
+
+        def gate_product(t):
             leave_bank(t, 1)
-            st2, gate = both[t][:, :S], both[t][:, S:]
-            other = sb("other%d" % t, [P, S], F32)
             if t == 0:
                 for c in range(HALVES):
                     nc.vector.tensor_tensor(
-                        st2[:, cols(c)], h_win[t][:].indirect(list_half(n2_sb, c)), gate[:, cols(c)], ALU.mult
+                        st2[t][:, cols(c)], h_win[t][:].indirect(list_half(n2_sb, c)), both[t][:, S:][:, cols(c)], ALU.mult
                     )
             else:
+                gate = y[:, t - 1, :]
                 for c in range(HALVES):
                     nc.scalar.activation(gate[:, cols(c)], h_win[t][:].indirect(list_half(n2_sb, c)), ACT.Sigmoid)
-                nc.vector.tensor_tensor(st2, h_ps[t][:], gate, ALU.mult)
-            if t < PACK - 1:
-                nc.vector.tensor_copy(other[:], both[t][:].indirect(n2_sb[:]))
-                nc.vector.tensor_tensor(y[:, t, :], st2, other[:], ALU.max)
-                nc.sync.dma_start(out_rows[:, t, :], y[:, t, :])
-            else:
-                for c in range(HALVES):
-                    nc.vector.tensor_copy(other[:, cols(c)], both[t][:].indirect(list_half(n2_sb, c)))
-                for c in range(HALVES):
-                    nc.vector.tensor_tensor(y[:, t, cols(c)], st2[:, cols(c)], other[:, cols(c)], ALU.max)
-                    nc.sync.dma_start(out_rows[:, t, cols(c)], y[:, t, cols(c)])
+                nc.vector.tensor_tensor(st2[t], h_ps[t][:], gate, ALU.mult)
+
+        gate_product(0)
+        for t in range(PACK - 1):
+            nc.vector.tensor_copy(other[t][:], both[t][:].indirect(n2_sb[:]))
+            gate_product(t + 1)
+            nc.vector.tensor_tensor(y[:, t, :], st2[t], other[t][:], ALU.max)
+            nc.sync.dma_start(out_rows[:, t, :], y[:, t, :])
+        t = PACK - 1
+        for c in range(HALVES):
+            nc.vector.tensor_copy(other[t][:, cols(c)], both[t][:].indirect(list_half(n2_sb, c)))
+        for c in range(HALVES):
+            nc.vector.tensor_tensor(y[:, t, cols(c)], st2[t][:, cols(c)], other[t][:, cols(c)], ALU.max)
+            nc.sync.dma_start(out_rows[:, t, cols(c)], y[:, t, cols(c)])
 
         y_scales = sb("y_scales", [P, S], U8)
         for c in range(HALVES):

@@ -44,9 +44,10 @@ def tile_picked_keytwicetwicp_none_po_kernel(
         def list_half(lst, c):
             return lst[:, c * LIST_COLS : (c + 1) * LIST_COLS]
 
-        def deal(dst, src):
+        def deal(dst, src, run):
             nc.vector.tensor_copy(
-                out=dst[:].rearrange("p (t m) -> p m t", t=PACK), in_=src[:].rearrange("p (m t) -> p m t", t=PACK)
+                out=dst[:].rearrange("p (t m i) -> p m t i", t=PACK, i=run),
+                in_=src[:].rearrange("p (m i t) -> p m t i", t=PACK, i=run),
             )
 
         def interleave_views(dst, src):
@@ -86,7 +87,7 @@ def tile_picked_keytwicetwicp_none_po_kernel(
         ds_got = sb("ds_got", [P, H], U8)
         nc.vector.tensor_copy(ds_got[:], ds_tab[:].indirect(kidx_sb[:]))
         ds_dealt = sb("ds_dealt", [P, H], U8)
-        deal(ds_dealt, ds_got)
+        deal(ds_dealt, ds_got, 16)
         for r in range(2):
             nc.scalar.dma_start(ds_dealt[2 + r : P : 32, :].bitcast(I32), ds_dealt[16 + r : P : 32, :].bitcast(I32))
         ws_raw = sb("ws_raw", [P, N], U8, tag="ds_got")
@@ -106,7 +107,10 @@ def tile_picked_keytwicetwicp_none_po_kernel(
         for c in range(HALVES):
             nc.vector.tensor_copy(x_got[:, cols(c)], x_tab[:].indirect(list_half(offs_sb, c)))
         d_rest = reuse.tile([P, PACK - 1, P], U32, name="d_rest", align_bytes=64, offset=5 * N)
-        nc.vector.tensor_copy(d_rest[:].rearrange("p t m -> p m t"), d_by_slot[:, :, 1:])
+        nc.vector.tensor_copy(
+            d_rest[:].rearrange("p t (m i) -> p m t i", i=4),
+            d_got[:].rearrange("p (m i t) -> p m t i", t=PACK, i=4)[:, :, 1:, :],
+        )
         d_stat = [d_first[:]] + [d_rest[:, t, :] for t in range(PACK - 1)]
 
         row_scale = sb("row_scale", [P, PACK], F32)
@@ -134,8 +138,8 @@ def tile_picked_keytwicetwicp_none_po_kernel(
 
         w_dealt = reuse.tile([P, N], U32, name="w_dealt", align_bytes=64, offset=0)
         ws_dealt = reuse.tile([P, N], U8, name="ws_dealt", align_bytes=64, offset=4 * N)
-        deal(w_dealt, w_raw)
-        deal(ws_dealt, ws_raw)
+        deal(w_dealt, w_raw, 4)
+        deal(ws_dealt, ws_raw, 16)
 
         s_tiles = [sb("s_win%d" % t, [P, S if t == 0 else 2 * S], F32) for t in range(PACK)]
         s_last = sb("s_last", [P, S], F32)
@@ -228,7 +232,7 @@ def tile_picked_keytwicetwicp_none_po_kernel(
                 gate = y[:, t - 1, :]
                 for c in range(HALVES):
                     nc.scalar.activation(gate[:, cols(c)], h_win[t][:].indirect(list_half(n2_sb, c)), ACT.Sigmoid)
-                nc.vector.tensor_tensor(st2[t], h_ps[t][:], gate, ALU.mult)
+                    nc.gpsimd.tensor_tensor(st2[t][:, cols(c)], h_win[t][:, cols(c)], gate[:, cols(c)], ALU.mult)
 
         gate_product(0)
         for t in range(PACK - 1):

from contextlib import ExitStack

import concourse.mybir as mybir

K, T, S, N, G, H = 512, 2048, 512, 512, 2048, 512
FLOPS = 2 * K * H * S + 2 * H * N * S

F32 = mybir.dt.float32
BF16 = mybir.dt.bfloat16
I32 = mybir.dt.int32
U32 = mybir.dt.uint32
U16 = mybir.dt.uint16
U8 = mybir.dt.uint8
FP8X4 = mybir.dt.float8_e4m3fn_x4
ACT = mybir.ActivationFunctionType
ALU = mybir.AluOpType

P = 128
PACK = 4
HALF = S // 2
HALVES = 2
LIST_COLS = HALF // 16


def words_view(dram_words):
    return dram_words[0].rearrange("p n t -> p (n t)").bitcast(I32)


def tile_picked_keytwicetwicp_none_po_kernel(
    tc, x_words, x_scales, d_words, d_scales, gn, w1_words, w1_scales, offs, kidx, n1, n2, out_0, out_1, out_2
):
    nc = tc.nc
    with ExitStack() as ctx:
        pool = ctx.enter_context(tc.tile_pool(name="sbuf", bufs=1))
        reuse = ctx.enter_context(tc.tile_pool(name="reuse", bufs=1))
        psum = ctx.enter_context(tc.psum_pool(name="psum", bufs=1))

        def sb(name, shape, dtype, tag=None):
            return pool.tile(shape, dtype, name=name, tag=tag or name, align_bytes=64)

        def cols(c):
            return slice(c * HALF, (c + 1) * HALF)

        def list_half(lst, c):
            return lst[:, c * LIST_COLS : (c + 1) * LIST_COLS]

        def deal(dst, src, run):
            nc.vector.tensor_copy(
                out=dst[:].rearrange("p (t m i) -> p m t i", t=PACK, i=run),
                in_=src[:].rearrange("p (m i t) -> p m t i", t=PACK, i=run),
            )

        def interleave_views(dst, src):
            return (
                dst[:].rearrange("p (c i t) -> p c t i", i=4, t=PACK),
                src.rearrange("p t (c i) -> p c t i", i=4),
            )

        kidx_sb = sb("kidx_sb", [P, H // 16], U16)
        offs_sb = sb("offs_sb", [P, S // 16], U16)
        n1_sb = sb("n1_sb", [P, S // 16], U16)
        n2_sb = sb("n2_sb", [P, S // 16], U16)
        d_tab = sb("d_tab", [P, G], U32)
        x_tab = reuse.tile([P, T], U32, name="x_tab", align_bytes=64, offset=0)
        ds_tab = sb("ds_tab", [P, G], U8)
        xs_tab = sb("xs_tab", [P, T], U8)
        gn_sb = sb("gn_sb", [P, PACK], F32)

        nc.vector.memset(ds_tab[:].bitcast(I32), 0)
        nc.gpsimd.memset(xs_tab[:].bitcast(I32), 0)

        nc.sync.dma_start(kidx_sb[:], kidx)
        nc.sync.dma_start(offs_sb[:], offs)
        nc.sync.dma_start(n1_sb[:], n1)
        nc.sync.dma_start(n2_sb[:], n2)
        nc.sync.dma_start(gn_sb[:], gn.rearrange("(p t) o -> p (t o)", t=PACK))
        d_rows = d_scales[0].rearrange("(a r) c -> r a c", r=2)
        for r in range(2):
            nc.sync.dma_start(ds_tab[r:P:16, :].bitcast(I32), d_rows[r].bitcast(I32))
        nc.sync.dma_start(d_tab[:].bitcast(I32), words_view(d_words))
        for q in range(4):
            nc.sync.dma_start(xs_tab[32 * q : 32 * q + 4, :].bitcast(I32), x_scales[0, 4 * q : 4 * q + 4, :].bitcast(I32))
        nc.sync.dma_start(x_tab[:].bitcast(I32), words_view(x_words))
        warm = sb("warm", [P, PACK], F32)
        nc.scalar.activation(warm[:], gn_sb[:], ACT.Sigmoid)

        ds_got = sb("ds_got", [P, H], U8)
        nc.vector.tensor_copy(ds_got[:], ds_tab[:].indirect(kidx_sb[:]))
        ds_dealt = sb("ds_dealt", [P, H], U8)
        deal(ds_dealt, ds_got, 16)
        for r in range(2):
            nc.scalar.dma_start(ds_dealt[2 + r : P : 32, :].bitcast(I32), ds_dealt[16 + r : P : 32, :].bitcast(I32))
        ws_raw = sb("ws_raw", [P, N], U8, tag="ds_got")
        nc.gpsimd.memset(ws_raw[:].bitcast(I32), 0)
        for q in range(4):
            nc.sync.dma_start(ws_raw[32 * q : 32 * q + 4, :].bitcast(I32), w1_scales[0, 4 * q : 4 * q + 4, :].bitcast(I32))
        xs_got = sb("xs_got", [P, S], U8)
        nc.vector.tensor_copy(xs_got[:], xs_tab[:].indirect(offs_sb[:]))
        d_got = sb("d_got", [P, H], U32)
        nc.vector.tensor_copy(d_got[:], d_tab[:].indirect(kidx_sb[:]))
        w_raw = sb("w_raw", [P, N], U32, tag="d_tab")
        nc.sync.dma_start(w_raw[:].bitcast(I32), words_view(w1_words))
        d_first = sb("d_first", [P, P], U32)
        d_by_slot = d_got[:].rearrange("p (m t) -> p m t", t=PACK)
        nc.vector.tensor_copy(d_first[:], d_by_slot[:, :, 0])
        x_got = sb("x_got", [P, S], U32)
        for c in range(HALVES):
            nc.vector.tensor_copy(x_got[:, cols(c)], x_tab[:].indirect(list_half(offs_sb, c)))
        d_rest = reuse.tile([P, PACK - 1, P], U32, name="d_rest", align_bytes=64, offset=5 * N)
        nc.vector.tensor_copy(
            d_rest[:].rearrange("p t (m i) -> p m t i", i=4),
            d_got[:].rearrange("p (m i t) -> p m t i", t=PACK, i=4)[:, :, 1:, :],
        )
        d_stat = [d_first[:]] + [d_rest[:, t, :] for t in range(PACK - 1)]

        row_scale = sb("row_scale", [P, PACK], F32)
        nc.scalar.activation(row_scale[:], gn_sb[:], ACT.Copy, scale=0.03125)

        s_first = psum.tile([P, HALF], F32, name="s_first")
        s_banks = [psum.tile([P, S], F32, name="s_bank%d" % t, tag="bank%d" % t) for t in range(PACK)]
        s_ps = {(0, 0): s_first[:], (0, 1): s_banks[0][:, cols(1)]}

        def scores(out, t, js):
            nc.tensor.matmul_mx(
                out=out,
                lhsT=d_stat[t].bitcast(FP8X4),
                lhsT_scale=ds_dealt[:, t * P : (t + 1) * P],
                rhs=x_got[:, js].bitcast(FP8X4),
                rhs_scale=xs_got[:, js],
                start=True,
                stop=True,
            )

        for c in range(HALVES):
            scores(s_ps[0, c], 0, cols(c))
        for t in range(1, PACK):
            scores(s_banks[t][:], t, slice(0, S))

        w_dealt = reuse.tile([P, N], U32, name="w_dealt", align_bytes=64, offset=0)
        ws_dealt = reuse.tile([P, N], U8, name="ws_dealt", align_bytes=64, offset=4 * N)
        deal(w_dealt, w_raw, 4)
        deal(ws_dealt, ws_raw, 16)

        s_tiles = [sb("s_win%d" % t, [P, S if t == 0 else 2 * S], F32) for t in range(PACK)]
        s_last = sb("s_last", [P, S], F32)
        s_win = [s_tiles[t][:, :S] for t in range(PACK)]
        s_dup = [s_tiles[t + 1][:, S:] for t in range(PACK - 1)] + [s_last[:]]
        m_win = [sb("m_win%d" % t, [P, S], F32) for t in range(PACK)]
        for t in range(PACK):
            scale = row_scale[:, t : t + 1]
            if t == 0:
                for c in range(HALVES):
                    for dst in (s_win, s_dup):
                        nc.scalar.activation(dst[t][:, cols(c)], s_ps[t, c], ACT.Copy, scale=scale)
            else:
                for dst in (s_win, s_dup):
                    nc.scalar.activation(dst[t], s_banks[t][:], ACT.Copy, scale=scale)
            if t == 0:
                for c in range(HALVES):
                    nc.vector.tensor_tensor(
                        m_win[t][:, cols(c)], s_tiles[t][:].indirect(list_half(n1_sb, c)), s_dup[t][:, cols(c)], ALU.subtract
                    )
            else:
                nc.vector.tensor_tensor(m_win[t][:], s_tiles[t][:].indirect(n1_sb[:]), s_dup[t], ALU.subtract)
        m_dbl = {}

        def double(t, c, dst):
            m_dbl[t, c] = dst
            nc.scalar.activation(dst, m_win[t][:, cols(c)], ACT.Copy, scale=2.0)

        both = [sb("both%d" % t, [P, 2 * S if t < PACK - 1 else S], F32) for t in range(PACK)]
        for t in range(PACK):
            double(t, 0, both[1 + t // 2][:, S:][:, cols(t % 2)])
        for t in range(2):
            double(t, 1, sb("m_dbl%d" % t, [P, HALF], F32)[:])

        h_ps = [psum.tile([P, S], F32, name="h_ps%d" % t, tag="bank%d" % ((t + 4) % 7)) for t in range(PACK)]
        h_win = [sb("h_win%d" % t, [P, S], F32) for t in range(PACK)]

        def leave_bank(t, c):
            if t == 0:
                nc.scalar.activation(h_win[t][:, cols(c)], h_ps[t][:, cols(c)], ACT.Sigmoid)
                nc.scalar.copy(both[t][:, S:][:, cols(c)], h_ps[t][:, cols(c)])
            else:
                nc.scalar.copy(h_win[t][:, cols(c)], h_ps[t][:, cols(c)])

        for c in range(HALVES):
            z = sb("z%d" % c, [P, PACK, HALF], F32)
            if c == 1:
                m_late = sb("m_late", [P, 2, HALF], F32, tag="z0")
                for t in (2, 3):
                    double(t, c, m_late[:, t - 2, :])
            for t in range(PACK):
                nc.vector.tensor_tensor(
                    z[:, t, :], m_win[t][:].indirect(list_half(n1_sb, c)), m_dbl[t, c], ALU.subtract
                )
            z_bf = sb("z_bf%d" % c, [P, HALF * PACK], BF16)
            dst, src = interleave_views(z_bf, z[:])
            if c == 0:
                nc.scalar.copy(dst, src)
            else:
                nc.vector.tensor_copy(dst, src)
            z_codes = sb("z_codes%d" % c, [P, HALF], U32)
            z_scales = sb("z_scales%d" % c, [P, HALF], U8)
            nc.vector.quantize_mx(out=z_codes[:].bitcast(FP8X4), scales=z_scales[:], in_=z_bf[:])
            for t in range(PACK):
                nc.tensor.matmul_mx(
                    out=h_ps[t][:, cols(c)],
                    lhsT=w_dealt[:, t * P : (t + 1) * P].bitcast(FP8X4),
                    lhsT_scale=ws_dealt[:, t * P : (t + 1) * P],
                    rhs=z_codes[:].bitcast(FP8X4),
                    rhs_scale=z_scales[:],
                    start=True,
                    stop=True,
                )
                if c == 0:
                    leave_bank(t, c)

        y = sb("y", [P, PACK, S], F32)
        out_rows = out_0.rearrange("(p t) j -> p t j", t=PACK)
        st2 = [both[t][:, :S] for t in range(PACK)]
        other = [sb("other%d" % t, [P, S], F32) for t in range(PACK)]

        def gate_product(t):
            leave_bank(t, 1)
            if t == 0:
                for c in range(HALVES):
                    nc.vector.tensor_tensor(
                        st2[t][:, cols(c)], h_win[t][:].indirect(list_half(n2_sb, c)), both[t][:, S:][:, cols(c)], ALU.mult
                    )
            else:
                gate = y[:, t - 1, :]
                for c in range(HALVES):
                    nc.scalar.activation(gate[:, cols(c)], h_win[t][:].indirect(list_half(n2_sb, c)), ACT.Sigmoid)
                    nc.gpsimd.tensor_tensor(st2[t][:, cols(c)], h_win[t][:, cols(c)], gate[:, cols(c)], ALU.mult)

        gate_product(0)
        for t in range(PACK - 1):
            nc.vector.tensor_copy(other[t][:], both[t][:].indirect(n2_sb[:]))
            gate_product(t + 1)
            nc.vector.tensor_tensor(y[:, t, :], st2[t], other[t][:], ALU.max)
            nc.sync.dma_start(out_rows[:, t, :], y[:, t, :])
        t = PACK - 1
        for c in range(HALVES):
            nc.vector.tensor_copy(other[t][:, cols(c)], both[t][:].indirect(list_half(n2_sb, c)))
        for c in range(HALVES):
            nc.vector.tensor_tensor(y[:, t, cols(c)], st2[t][:, cols(c)], other[t][:, cols(c)], ALU.max)
            nc.sync.dma_start(out_rows[:, t, cols(c)], y[:, t, cols(c)])

        y_scales = sb("y_scales", [P, S], U8)
        for c in range(HALVES):
            y_bf = sb("y_bf%d" % c, [P, HALF * PACK], BF16)
            dst, src = interleave_views(y_bf, y[:, :, cols(c)])
            if c == 0:
                nc.scalar.copy(dst, src)
            else:
                nc.vector.tensor_copy(dst, src)
            y_codes = sb("y_codes%d" % c, [P, HALF], U32)
            nc.vector.quantize_mx(out=y_codes[:].bitcast(FP8X4), scales=y_scales[:, cols(c)], in_=y_bf[:])
            nc.sync.dma_start(words_view(out_1)[:, cols(c)], y_codes[:].bitcast(I32))
        for q in range(4):
            eng = nc.scalar if q % 2 == 0 else nc.sync
            eng.dma_start(out_2[0, 4 * q : 4 * q + 4, :].bitcast(I32), y_scales[32 * q : 32 * q + 4, :].bitcast(I32))
